import numpy as np
import ml_dtypes


def mxq(x, axis, fmt="e4m3"):
    dtype, down = {"e4m3": (ml_dtypes.float8_e4m3fn, 7), "e5m2": (ml_dtypes.float8_e5m2, 14)}[fmt]
    v = np.moveaxis(np.asarray(x, np.float32).astype(ml_dtypes.bfloat16).astype(np.float64), axis, -1)
    blocks = v.reshape(v.shape[:-1] + (-1, 32))
    amax = np.abs(blocks).max(-1, keepdims=True)
    byte = np.maximum(np.where(amax > 0, np.frexp(amax)[1] - 1 + 127, 0) - down, 1)
    scale = np.exp2(byte - 127.0)
    codes = (blocks / scale).astype(np.float32).astype(dtype).astype(np.float64)
    return np.moveaxis((codes * scale).reshape(v.shape), -1, axis)


WIDE = False


def mx_kscale(k):
    if not WIDE:
        return np.ones(k)
    levels = np.array([24, -24, 12, -12, 0])
    if k % 512:
        return np.exp2(np.random.permutation(np.resize(levels, k // 32))).repeat(32)
    a = np.empty((k // 512, 16))
    for p in range(k // 512):
        a[p, :8] = np.random.permutation(np.resize(levels, 8))
        for g in range(8):
            far = levels[np.abs(levels - a[p, g]) >= 10]
            a[p, g + 8] = far[np.random.randint(len(far))]
    return np.exp2(a.ravel()).repeat(32)


def f64(x):
    return np.asarray(x).astype(np.float64)


def striped8(idx):
    return np.concatenate([v.reshape(-1, 16).T for v in idx]).astype(np.uint16)


def unstriped8(offs):
    return np.stack([offs[16 * g:16 * g + 16].T.reshape(-1) for g in range(8)]).astype(np.int64)


E2M1 = np.array([0.0, 0.5, 1.0, 1.5, 2.0, 3.0, 4.0, 6.0, -0.0, -0.5, -1.0, -1.5, -2.0, -3.0, -4.0, -6.0])


def pack_weight(w, fmt):
    k, n = w.shape
    w = f64(np.asarray(w, np.float32).astype(ml_dtypes.bfloat16)).reshape(k // 32, 32, n)
    amax = np.abs(w).max(1)
    if fmt == "e4m3":
        byte = np.frexp(amax)[1] - 1 + 127 - 7
    else:
        mant, ex = np.frexp(amax / 6.0)
        byte = np.where(mant > 0.5, ex, ex - 1) + 127
    byte = np.clip(np.where(amax > 0, byte, 1), 1, 254)
    scaled = (w * np.exp2(127.0 - byte)[:, None, :]).reshape(k, n).astype(np.float32)
    by_word = np.ascontiguousarray(scaled.reshape(k // 512, 128, 4, n).transpose(0, 1, 3, 2))
    if fmt == "e4m3":
        words = by_word.astype(ml_dtypes.float8_e4m3fn).view(np.uint8)
    else:
        c = by_word.astype(ml_dtypes.float4_e2m1fn).view(np.uint8) & 0xF
        words = (c[..., 0::2] | (c[..., 1::2] << 4)).reshape(k // 512, 128, 2 * n)
    return np.ascontiguousarray(words), np.ascontiguousarray(byte.astype(np.uint8).reshape(k // 512, 16, n))


def unpack_weight(words, scales, fmt):
    g, _, n = scales.shape
    words = np.ascontiguousarray(words).reshape(g, 128, n, -1)
    if fmt == "e4m3":
        vals = words.view(ml_dtypes.float8_e4m3fn).astype(np.float64)
    else:
        nib = np.empty((g, 128, n, 4), np.uint8)
        nib[..., 0::2] = words & 0xF
        nib[..., 1::2] = words >> 4
        vals = E2M1[nib]
    vals = vals * np.repeat(np.exp2(scales.astype(np.float64) - 127.0), 8, axis=1)[..., None]
    return vals.transpose(0, 1, 3, 2).reshape(g * 512, n)


def sigm(f):
    return 1.0 / (1.0 + np.exp(-np.maximum(f, -700.0)))


K, L, N, T, J = 512, 512, 512, 2048, 1024


def setup_inputs():
    n = np.random.standard_normal
    s = mx_kscale(K)[:, None]
    s2 = mx_kscale(L)[:, None]
    p_wa = pack_weight(n((K, N)) / np.sqrt(K) / s, "e2m1")
    p_wb = pack_weight(n((L, N)) / np.sqrt(L) / s2, "e4m3")
    return {
        "xT": (n((K, T)) * s).astype(np.float32),
        "wgt": np.repeat(np.random.uniform(0.5, 2.0, (8, J)), 16, axis=0).astype(np.float32),
        "zT": (n((L, T)) * s2).astype(np.float32),
        "wgt2": np.repeat(np.random.uniform(0.5, 2.0, (8, J)), 16, axis=0).astype(np.float32),
        "wa_words": p_wa[0],
        "wa_scales": p_wa[1],
        "wb_words": p_wb[0],
        "wb_scales": p_wb[1],
        "offs": striped8(np.stack([np.random.permutation(T)[:J] for _ in range(8)])),
        "offs2": striped8(np.stack([np.random.permutation(T)[:J] for _ in range(8)])),
    }


def reference(xT, wgt, zT, wgt2, wa_words, wa_scales, wb_words, wb_scales, offs, offs2):
    idx = unstriped8(offs)
    idx2 = unstriped8(offs2)
    rows = np.arange(K)
    xg = f64(wgt)[rows // 4 % 128] * f64(xT)[rows[:, None], idx[rows % 512 // 64]]
    xT_ = mxq(xg, 0, "e4m3")
    rows = np.arange(L)
    xg = f64(wgt2)[rows // 4 % 128] * f64(zT)[rows[:, None], idx2[rows % 512 // 64]]
    zT_ = mxq(xg, 0, "e4m3")
    wa_ = unpack_weight(wa_words, wa_scales, "e2m1")
    wb_ = unpack_weight(wb_words, wb_scales, "e4m3")
    ya = wa_.T @ xT_
    yb = wb_.T @ zT_
    return ya * sigm(yb)

@@ -1,0 +1,158 @@
+from contextlib import ExitStack
+
+import concourse.mybir as mybir
+
+K, N, T, J = 512, 512, 2048, 1024
+FLOPS = 2 * 2 * K * N * J
+
+F32 = mybir.dt.float32
+BF16 = mybir.dt.bfloat16
+I32 = mybir.dt.int32
+U32 = mybir.dt.uint32
+U16 = mybir.dt.uint16
+U8 = mybir.dt.uint8
+FP8X4 = mybir.dt.float8_e4m3fn_x4
+FP4X4 = mybir.dt.float4_e2m1fn_x4
+MULT = mybir.AluOpType.mult
+SIGMOID = mybir.ActivationFunctionType.Sigmoid
+
+P = 128
+PACK = 4
+N_TILES = N // P
+BANK = 512
+HALF = J // 2
+Z_CHUNKS = [256, 256, 256, 256]
+X_CHUNKS = [128, 128, 256, 256, 256]
+
+
+def spans(widths):
+    starts = [sum(widths[:i]) for i in range(len(widths))]
+    return [slice(s, s + w) for s, w in zip(starts, widths)]
+
+
+def tile_list_gate_none_kernel(
+    tc, xT, wgt, zT, wgt2, wa_words, wa_scales, wb_words, wb_scales, offs, offs2, out
+):
+    nc = tc.nc
+    halves = spans([HALF, HALF])
+    out_v = out.rearrange("(t p) j -> p t j", p=P)
+
+    with ExitStack() as ctx:
+        keep = ctx.enter_context(tc.tile_pool(name="keep", bufs=1))
+        psum = ctx.enter_context(tc.psum_pool(name="psum", bufs=8))
+
+        x_list = keep.tile([P, J // 16], U16, name="x_list")
+        z_list = keep.tile([P, J // 16], U16, name="z_list")
+        x_wgt = keep.tile([P, J], F32, name="x_wgt")
+        z_wgt = keep.tile([P, J], F32, name="z_wgt")
+        x_planes = [keep.tile([P, T], F32, name="x_plane%d" % i) for i in range(PACK)]
+        z_planes = [keep.tile([P, T], F32, name="z_plane%d" % i) for i in range(PACK)]
+        x_picked = keep.tile([P, PACK, J], F32, name="x_picked")
+        z_picked = keep.tile([P, PACK, J], F32, name="z_picked")
+        x_grouped = keep.tile([P, J, PACK], BF16, name="x_grouped", align_bytes=64)
+        z_grouped = keep.tile([P, J, PACK], BF16, name="z_grouped", align_bytes=64)
+        x_codes = keep.tile([P, J], U32, name="x_codes", align_bytes=64)
+        z_codes = keep.tile([P, J], U32, name="z_codes", align_bytes=64)
+        x_scale = keep.tile([P, J], U8, name="x_scale", align_bytes=64)
+        z_scale = keep.tile([P, J], U8, name="z_scale", align_bytes=64)
+        wa_codes = keep.tile([P, 2 * N], U8, name="wa_codes", align_bytes=64)
+        wb_codes = keep.tile([P, 4 * N], U8, name="wb_codes", align_bytes=64)
+        wa_scale = keep.tile([P, N], U8, name="wa_scale", align_bytes=64)
+        wb_scale = keep.tile([P, N], U8, name="wb_scale", align_bytes=64)
+        gate = keep.tile([P, N_TILES, J], F32, name="gate")
+        result = keep.tile([P, N_TILES, J], F32, name="result")
+
+        x_rows = xT.rearrange("(p i) t -> p i t", i=PACK)
+        z_rows = zT.rearrange("(p i) t -> p i t", i=PACK)
+
+        for plane, rows in ((wb_scale, wb_scales), (wa_scale, wa_scales)):
+            nc.gpsimd.memset(plane[:].bitcast(I32), 0)
+            for q in range(4):
+                nc.gpsimd.dma_start(
+                    out=plane[32 * q : 32 * q + 4, :].bitcast(I32),
+                    in_=rows[0, 4 * q : 4 * q + 4, :].bitcast(I32),
+                )
+
+        nc.sync.dma_start(z_list[:], offs2)
+        nc.sync.dma_start(out=z_wgt[:], in_=wgt2)
+        for i in range(PACK):
+            nc.sync.dma_start(out=z_planes[i][:], in_=z_rows[:, i, :])
+        nc.sync.dma_start(x_list[:], offs)
+        nc.sync.dma_start(out=x_wgt[:, halves[0]], in_=wgt[:, halves[0]])
+        nc.sync.dma_start(out=x_planes[0][:], in_=x_rows[:, 0, :])
+        nc.sync.dma_start(out=x_wgt[:, halves[1]], in_=wgt[:, halves[1]])
+        nc.sync.dma_start(
+            out=wb_codes[:].bitcast(I32),
+            in_=wb_words[0].rearrange("p n t -> p (n t)").bitcast(I32),
+        )
+        for i in range(1, PACK):
+            nc.sync.dma_start(out=x_planes[i][:], in_=x_rows[:, i, :])
+        nc.sync.dma_start(out=wa_codes[:].bitcast(I32), in_=wa_words[0].bitcast(I32))
+
+        def gather(picked, planes, lists, weights, i, cols):
+            window = planes[i][:].indirect(lists[:, cols.start // 16 : cols.stop // 16])
+            nc.vector.tensor_tensor(picked[:, i, cols], window, weights[:, cols], MULT)
+
+        def interleave(grouped, picked, cols):
+            nc.scalar.copy(
+                grouped[:, cols, :].rearrange("p (c e) i -> p c i e", e=4),
+                picked[:, :, cols].rearrange("p i (c e) -> p c i e", e=4),
+            )
+
+        def quantize(codes, scale, grouped, cols):
+            nc.vector.quantize_mx(
+                out=codes[:, cols].bitcast(FP8X4),
+                scales=scale[:, cols],
+                in_=grouped[:, cols, :].rearrange("p c i -> p (c i)"),
+            )
+
+        def project(w_codes, w_dtype, w_scale, codes, scale, cols):
+            width = cols.stop - cols.start
+            per_bank = BANK // width
+            w_bytes = w_codes.shape[1] // N_TILES
+            banks = []
+            for t0 in range(0, N_TILES, per_bank):
+                bank = psum.tile([P, per_bank, width], F32, name="bank")
+                for t in range(t0, t0 + per_bank):
+                    nc.tensor.matmul_mx(
+                        out=bank[:, t - t0, :],
+                        lhsT=w_codes[:, t * w_bytes : (t + 1) * w_bytes].bitcast(w_dtype),
+                        lhsT_scale=w_scale[:, t * P : (t + 1) * P],
+                        rhs=codes[:, cols].bitcast(FP8X4),
+                        rhs_scale=scale[:, cols],
+                        start=True,
+                        stop=True,
+                    )
+                banks.append((bank, slice(t0, t0 + per_bank)))
+            return banks
+
+        def gate_chunk(cols):
+            quantize(z_codes, z_scale, z_grouped, cols)
+            for bank, tiles in project(wb_codes, FP8X4, wb_scale, z_codes, z_scale, cols):
+                nc.scalar.activation(gate[:, tiles, cols], bank[:], SIGMOID)
+
+        for i in range(PACK - 1):
+            for cols in halves:
+                gather(z_picked, z_planes, z_list, z_wgt, i, cols)
+        z_spans = spans(Z_CHUNKS)
+        for cols in z_spans:
+            gather(z_picked, z_planes, z_list, z_wgt, PACK - 1, cols)
+            interleave(z_grouped, z_picked, cols)
+
+        gather(x_picked, x_planes, x_list, x_wgt, 0, halves[0])
+        gate_chunk(z_spans[0])
+        gate_chunk(z_spans[1])
+        gather(x_picked, x_planes, x_list, x_wgt, 0, halves[1])
+        gate_chunk(z_spans[2])
+        gate_chunk(z_spans[3])
+        for i in range(1, PACK - 1):
+            for cols in halves:
+                gather(x_picked, x_planes, x_list, x_wgt, i, cols)
+
+        for cols in spans(X_CHUNKS):
+            gather(x_picked, x_planes, x_list, x_wgt, PACK - 1, cols)
+            interleave(x_grouped, x_picked, cols)
+            quantize(x_codes, x_scale, x_grouped, cols)
+            for bank, tiles in project(wa_codes, FP4X4, wa_scale, x_codes, x_scale, cols):
+                nc.vector.tensor_tensor(result[:, tiles, cols], bank[:], gate[:, tiles, cols], MULT)
+                nc.sync.dma_start(out=out_v[:, tiles, cols], in_=result[:, tiles, cols])

@@ -59,19 +59,25 @@ def tile_list_gate_none_kernel(
         wb_codes = keep.tile([P, 4 * N], U8, name="wb_codes", align_bytes=64)
         wa_scale = keep.tile([P, N], U8, name="wa_scale", align_bytes=64)
         wb_scale = keep.tile([P, N], U8, name="wb_scale", align_bytes=64)
+        warm = keep.tile([P, 16], F32, name="warm")
         gate = keep.tile([P, N_TILES, J], F32, name="gate")
         result = keep.tile([P, N_TILES, J], F32, name="result")
 
         x_rows = xT.rearrange("(p i) t -> p i t", i=PACK)
         z_rows = zT.rearrange("(p i) t -> p i t", i=PACK)
 
-        for plane, rows in ((wb_scale, wb_scales), (wa_scale, wa_scales)):
-            nc.gpsimd.memset(plane[:].bitcast(I32), 0)
+        def load_scales(queue, plane, rows):
             for q in range(4):
-                nc.gpsimd.dma_start(
+                queue.dma_start(
                     out=plane[32 * q : 32 * q + 4, :].bitcast(I32),
                     in_=rows[0, 4 * q : 4 * q + 4, :].bitcast(I32),
                 )
+
+        nc.vector.memset(wb_scale[:].bitcast(I32), 0)
+        nc.vector.memset(wa_scale[:].bitcast(I32), 0)
+        nc.vector.memset(warm[:, 0:1], 0.0)
+        nc.scalar.activation(warm[:, 8:9], warm[:, 0:1], SIGMOID)
+        load_scales(nc.gpsimd, wb_scale, wb_scales)
 
         nc.sync.dma_start(z_list[:], offs2)
         nc.sync.dma_start(out=z_wgt[:], in_=wgt2)
@@ -88,6 +94,7 @@ def tile_list_gate_none_kernel(
         for i in range(1, PACK):
             nc.sync.dma_start(out=x_planes[i][:], in_=x_rows[:, i, :])
         nc.sync.dma_start(out=wa_codes[:].bitcast(I32), in_=wa_words[0].bitcast(I32))
+        load_scales(nc.sync, wa_scale, wa_scales)
 
         def gather(picked, planes, lists, weights, i, cols):
             window = planes[i][:].indirect(lists[:, cols.start // 16 : cols.stop // 16])
@@ -139,20 +146,28 @@ def tile_list_gate_none_kernel(
             gather(z_picked, z_planes, z_list, z_wgt, PACK - 1, cols)
             interleave(z_grouped, z_picked, cols)
 
-        gather(x_picked, x_planes, x_list, x_wgt, 0, halves[0])
-        gate_chunk(z_spans[0])
-        gate_chunk(z_spans[1])
-        gather(x_picked, x_planes, x_list, x_wgt, 0, halves[1])
-        gate_chunk(z_spans[2])
-        gate_chunk(z_spans[3])
-        for i in range(1, PACK - 1):
-            for cols in halves:
-                gather(x_picked, x_planes, x_list, x_wgt, i, cols)
+        x_early = [(i, cols) for i in range(PACK - 1) for cols in halves]
+        gates_after = {0: z_spans[0:2], 1: z_spans[2:3], 2: z_spans[3:4]}
+        for step, (i, cols) in enumerate(x_early):
+            gather(x_picked, x_planes, x_list, x_wgt, i, cols)
+            for z_cols in gates_after.get(step, []):
+                gate_chunk(z_cols)
 
-        for cols in spans(X_CHUNKS):
+        x_spans = spans(X_CHUNKS)
+        for cols in x_spans:
             gather(x_picked, x_planes, x_list, x_wgt, PACK - 1, cols)
             interleave(x_grouped, x_picked, cols)
-            quantize(x_codes, x_scale, x_grouped, cols)
-            for bank, tiles in project(wa_codes, FP4X4, wa_scale, x_codes, x_scale, cols):
+
+        def finish(banks, cols):
+            for bank, tiles in banks:
                 nc.vector.tensor_tensor(result[:, tiles, cols], bank[:], gate[:, tiles, cols], MULT)
                 nc.sync.dma_start(out=out_v[:, tiles, cols], in_=result[:, tiles, cols])
+
+        pending = None
+        for cols in x_spans:
+            quantize(x_codes, x_scale, x_grouped, cols)
+            banks = project(wa_codes, FP4X4, wa_scale, x_codes, x_scale, cols)
+            if pending is not None:
+                finish(*pending)
+            pending = (banks, cols)
+        finish(*pending)

@@ -23,6 +23,8 @@ BANK = 512
 HALF = J // 2
 Z_CHUNKS = [256, 256, 256, 256]
 X_CHUNKS = [128, 128, 256, 256, 256]
+Z_FIRST_GATHERS = [256, 768]
+X_LAST_GATHERS = [128, 128, 256, 256, 256]
 
 
 def spans(widths):
@@ -77,20 +79,23 @@ def tile_list_gate_none_kernel(
         nc.vector.memset(wa_scale[:].bitcast(I32), 0)
         nc.vector.memset(warm[:, 0:1], 0.0)
         nc.scalar.activation(warm[:, 8:9], warm[:, 0:1], SIGMOID)
-        load_scales(nc.gpsimd, wb_scale, wb_scales)
+        load_scales(nc.scalar, wb_scale, wb_scales)
 
         nc.sync.dma_start(z_list[:], offs2)
-        nc.sync.dma_start(out=z_wgt[:], in_=wgt2)
-        for i in range(PACK):
+        first = spans(Z_FIRST_GATHERS)
+        nc.sync.dma_start(out=z_wgt[:, first[0]], in_=wgt2[:, first[0]])
+        nc.sync.dma_start(out=z_planes[0][:], in_=z_rows[:, 0, :])
+        nc.sync.dma_start(out=z_wgt[:, first[1]], in_=wgt2[:, first[1]])
+        for i in range(1, PACK):
             nc.sync.dma_start(out=z_planes[i][:], in_=z_rows[:, i, :])
         nc.sync.dma_start(x_list[:], offs)
         nc.sync.dma_start(out=x_wgt[:, halves[0]], in_=wgt[:, halves[0]])
         nc.sync.dma_start(out=x_planes[0][:], in_=x_rows[:, 0, :])
-        nc.sync.dma_start(out=x_wgt[:, halves[1]], in_=wgt[:, halves[1]])
         nc.sync.dma_start(
             out=wb_codes[:].bitcast(I32),
             in_=wb_words[0].rearrange("p n t -> p (n t)").bitcast(I32),
         )
+        nc.sync.dma_start(out=x_wgt[:, halves[1]], in_=wgt[:, halves[1]])
         for i in range(1, PACK):
             nc.sync.dma_start(out=x_planes[i][:], in_=x_rows[:, i, :])
         nc.sync.dma_start(out=wa_codes[:].bitcast(I32), in_=wa_words[0].bitcast(I32))
@@ -139,35 +144,53 @@ def tile_list_gate_none_kernel(
                 nc.scalar.activation(gate[:, tiles, cols], bank[:], SIGMOID)
 
         for i in range(PACK - 1):
-            for cols in halves:
+            for cols in first if i == 0 else halves:
                 gather(z_picked, z_planes, z_list, z_wgt, i, cols)
         z_spans = spans(Z_CHUNKS)
         for cols in z_spans:
             gather(z_picked, z_planes, z_list, z_wgt, PACK - 1, cols)
             interleave(z_grouped, z_picked, cols)
+        gate_chunk(z_spans[0])
 
         x_early = [(i, cols) for i in range(PACK - 1) for cols in halves]
-        gates_after = {0: z_spans[0:2], 1: z_spans[2:3], 2: z_spans[3:4]}
+        gates_after = {0: z_spans[1:2], 1: z_spans[2:4]}
         for step, (i, cols) in enumerate(x_early):
             gather(x_picked, x_planes, x_list, x_wgt, i, cols)
             for z_cols in gates_after.get(step, []):
                 gate_chunk(z_cols)
 
         x_spans = spans(X_CHUNKS)
-        for cols in x_spans:
-            gather(x_picked, x_planes, x_list, x_wgt, PACK - 1, cols)
-            interleave(x_grouped, x_picked, cols)
+        x_banks = []
 
-        def finish(banks, cols):
-            for bank, tiles in banks:
-                nc.vector.tensor_tensor(result[:, tiles, cols], bank[:], gate[:, tiles, cols], MULT)
-                nc.sync.dma_start(out=out_v[:, tiles, cols], in_=result[:, tiles, cols])
-
-        pending = None
-        for cols in x_spans:
+        def multiply_chunk(cols):
             quantize(x_codes, x_scale, x_grouped, cols)
-            banks = project(wa_codes, FP4X4, wa_scale, x_codes, x_scale, cols)
-            if pending is not None:
-                finish(*pending)
-            pending = (banks, cols)
-        finish(*pending)
+            for bank, tiles in project(wa_codes, FP4X4, wa_scale, x_codes, x_scale, cols):
+                x_banks.append((bank, tiles, cols))
+
+        def finish(bank, tiles, cols, pieces=1):
+            step = (tiles.stop - tiles.start) // pieces
+            for t0 in range(tiles.start, tiles.stop, step):
+                part = slice(t0, t0 + step)
+                sums = bank[:, t0 - tiles.start : t0 - tiles.start + step, :]
+                nc.vector.tensor_tensor(result[:, part, cols], sums, gate[:, part, cols], MULT)
+                nc.sync.dma_start(out=out_v[:, part, cols], in_=result[:, part, cols])
+
+        last = spans(X_LAST_GATHERS)
+        for cols in last[:-1]:
+            gather(x_picked, x_planes, x_list, x_wgt, PACK - 1, cols)
+        for cols in x_spans[:-1]:
+            interleave(x_grouped, x_picked, cols)
+        multiply_chunk(x_spans[0])
+        gather(x_picked, x_planes, x_list, x_wgt, PACK - 1, last[-1])
+        interleave(x_grouped, x_picked, x_spans[-1])
+        multiply_chunk(x_spans[1])
+        finish(*x_banks[0])
+        multiply_chunk(x_spans[2])
+        finish(*x_banks[1])
+        multiply_chunk(x_spans[3])
+        finish(*x_banks[2])
+        finish(*x_banks[3])
+        multiply_chunk(x_spans[4])
+        for item in x_banks[4:-1]:
+            finish(*item)
+        finish(*x_banks[-1], pieces=2)

@@ -1,6 +1,7 @@
 from contextlib import ExitStack
 
 import concourse.mybir as mybir
+from concourse.masks import make_identity
 
 K, N, T, J = 512, 512, 2048, 1024
 FLOPS = 2 * 2 * K * N * J
@@ -22,9 +23,11 @@ N_TILES = N // P
 BANK = 512
 HALF = J // 2
 Z_CHUNKS = [256, 256, 256, 256]
-X_CHUNKS = [128, 128, 256, 256, 256]
-Z_FIRST_GATHERS = [256, 768]
-X_LAST_GATHERS = [128, 128, 256, 256, 256]
+X_CHUNKS = [256, 256, 256, 256]
+Z_FIRST_GATHERS = [256, 256, 512]
+HEADS = 8
+GROUP = P // HEADS
+BLOCKS = J // P
 
 
 def spans(widths):
@@ -45,11 +48,11 @@ def tile_list_gate_none_kernel(
 
         x_list = keep.tile([P, J // 16], U16, name="x_list")
         z_list = keep.tile([P, J // 16], U16, name="z_list")
-        x_wgt = keep.tile([P, J], F32, name="x_wgt")
+        x_wgt_late = keep.tile([P, HALF], F32, name="x_wgt_late")
         z_wgt = keep.tile([P, J], F32, name="z_wgt")
         x_planes = [keep.tile([P, T], F32, name="x_plane%d" % i) for i in range(PACK)]
         z_planes = [keep.tile([P, T], F32, name="z_plane%d" % i) for i in range(PACK)]
-        x_picked = keep.tile([P, PACK, J], F32, name="x_picked")
+        x_picked = [keep.tile([P, PACK, HALF], F32, name="x_picked%d" % h) for h in range(2)]
         z_picked = keep.tile([P, PACK, J], F32, name="z_picked")
         x_grouped = keep.tile([P, J, PACK], BF16, name="x_grouped", align_bytes=64)
         z_grouped = keep.tile([P, J, PACK], BF16, name="z_grouped", align_bytes=64)
@@ -61,6 +64,10 @@ def tile_list_gate_none_kernel(
         wb_codes = keep.tile([P, 4 * N], U8, name="wb_codes", align_bytes=64)
         wa_scale = keep.tile([P, N], U8, name="wa_scale", align_bytes=64)
         wb_scale = keep.tile([P, N], U8, name="wb_scale", align_bytes=64)
+        z_head = keep.tile([P, Z_FIRST_GATHERS[0]], F32, name="z_head")
+        seed = keep.tile([P, P], F32, name="seed")
+        ident = keep.tile([P, P], F32, name="ident")
+        spread = keep.tile([P, BLOCKS, HEADS, GROUP], F32, name="spread")
         warm = keep.tile([P, 16], F32, name="warm")
         gate = keep.tile([P, N_TILES, J], F32, name="gate")
         result = keep.tile([P, N_TILES, J], F32, name="result")
@@ -78,38 +85,69 @@ def tile_list_gate_none_kernel(
         nc.vector.memset(wb_scale[:].bitcast(I32), 0)
         nc.vector.memset(wa_scale[:].bitcast(I32), 0)
         nc.vector.memset(warm[:, 0:1], 0.0)
-        nc.scalar.activation(warm[:, 8:9], warm[:, 0:1], SIGMOID)
-        load_scales(nc.scalar, wb_scale, wb_scales)
+        make_identity(nc, ident[:])
 
-        nc.sync.dma_start(z_list[:], offs2)
         first = spans(Z_FIRST_GATHERS)
-        nc.sync.dma_start(out=z_wgt[:, first[0]], in_=wgt2[:, first[0]])
+        for s, source in enumerate((wgt2, wgt)):
+            rows = source.rearrange("(g r) (b c) -> r g b c", r=GROUP, c=P)[0]
+            nc.sync.dma_start(out=seed[64 * s : 64 * (s + 1), :], in_=rows)
+        nc.scalar.activation(warm[:, 8:9], warm[:, 0:1], SIGMOID)
         nc.sync.dma_start(out=z_planes[0][:], in_=z_rows[:, 0, :])
-        nc.sync.dma_start(out=z_wgt[:, first[1]], in_=wgt2[:, first[1]])
+        nc.sync.dma_start(z_list[:], offs2)
+        nc.sync.dma_start(out=z_head[:], in_=wgt2[:, first[0]])
         for i in range(1, PACK):
             nc.sync.dma_start(out=z_planes[i][:], in_=z_rows[:, i, :])
         nc.sync.dma_start(x_list[:], offs)
-        nc.sync.dma_start(out=x_wgt[:, halves[0]], in_=wgt[:, halves[0]])
         nc.sync.dma_start(out=x_planes[0][:], in_=x_rows[:, 0, :])
         nc.sync.dma_start(
             out=wb_codes[:].bitcast(I32),
             in_=wb_words[0].rearrange("p n t -> p (n t)").bitcast(I32),
         )
-        nc.sync.dma_start(out=x_wgt[:, halves[1]], in_=wgt[:, halves[1]])
+        load_scales(nc.sync, wb_scale, wb_scales)
         for i in range(1, PACK):
             nc.sync.dma_start(out=x_planes[i][:], in_=x_rows[:, i, :])
         nc.sync.dma_start(out=wa_codes[:].bitcast(I32), in_=wa_words[0].bitcast(I32))
         load_scales(nc.sync, wa_scale, wa_scales)
 
-        def gather(picked, planes, lists, weights, i, cols):
-            window = planes[i][:].indirect(lists[:, cols.start // 16 : cols.stop // 16])
-            nc.vector.tensor_tensor(picked[:, i, cols], window, weights[:, cols], MULT)
+        turned = psum.tile([P, P], F32, name="bank")
+        nc.tensor.transpose(turned[:], seed[:], ident[:])
+        by_block = turned[:].rearrange("c (s g b) -> c s b g", s=2, g=HEADS)
+        x_wgt = [x_picked[1][:, PACK - 2, :], x_wgt_late[:]]
+        for s, weights in enumerate(([z_wgt[:, cols] for cols in halves], x_wgt)):
+            for blocks in spans([BLOCKS // 2] * 2):
+                nc.scalar.copy(
+                    spread[:, blocks],
+                    by_block[:, s, blocks].unsqueeze(3).to_broadcast([P, BLOCKS // 2, HEADS, GROUP]),
+                )
+            for h, blocks in enumerate(spans([BLOCKS // 2] * 2)):
+                bank = psum.tile([P, BLOCKS // 2, P], F32, name="bank")
+                for b in range(blocks.start, blocks.stop):
+                    nc.tensor.transpose(
+                        bank[:, b - blocks.start, :],
+                        spread[:, b].rearrange("c g r -> c (g r)"),
+                        ident[:],
+                    )
+                nc.scalar.copy(weights[h], bank[:].rearrange("p b c -> p (b c)"))
 
-        def interleave(grouped, picked, cols):
+        def gather(picked, planes, lists, weights, i, cols, base=0):
+            window = planes[i][:].indirect(lists[:, cols.start // 16 : cols.stop // 16])
+            local = slice(cols.start - base, cols.stop - base)
+            nc.vector.tensor_tensor(picked[:, i, local], window, weights[:, local], MULT)
+
+        def interleave(grouped, picked, cols, base=0):
+            local = slice(cols.start - base, cols.stop - base)
             nc.scalar.copy(
                 grouped[:, cols, :].rearrange("p (c e) i -> p c i e", e=4),
-                picked[:, :, cols].rearrange("p i (c e) -> p c i e", e=4),
+                picked[:, :, local].rearrange("p i (c e) -> p c i e", e=4),
             )
+
+        def gather_x(i, cols):
+            h = cols.start // HALF
+            gather(x_picked[h], x_planes, x_list, x_wgt[h], i, cols, h * HALF)
+
+        def interleave_x(cols):
+            h = cols.start // HALF
+            interleave(x_grouped, x_picked[h], cols, h * HALF)
 
         def quantize(codes, scale, grouped, cols):
             nc.vector.quantize_mx(
@@ -143,8 +181,9 @@ def tile_list_gate_none_kernel(
             for bank, tiles in project(wb_codes, FP8X4, wb_scale, z_codes, z_scale, cols):
                 nc.scalar.activation(gate[:, tiles, cols], bank[:], SIGMOID)
 
+        gather(z_picked, z_planes, z_list, z_head, 0, first[0])
         for i in range(PACK - 1):
-            for cols in first if i == 0 else halves:
+            for cols in first[1:] if i == 0 else [slice(0, J)]:
                 gather(z_picked, z_planes, z_list, z_wgt, i, cols)
         z_spans = spans(Z_CHUNKS)
         for cols in z_spans:
@@ -152,10 +191,10 @@ def tile_list_gate_none_kernel(
             interleave(z_grouped, z_picked, cols)
         gate_chunk(z_spans[0])
 
-        x_early = [(i, cols) for i in range(PACK - 1) for cols in halves]
+        x_early = [(i, cols) for i in range(PACK - 2) for cols in halves]
         gates_after = {0: z_spans[1:2], 1: z_spans[2:4]}
         for step, (i, cols) in enumerate(x_early):
-            gather(x_picked, x_planes, x_list, x_wgt, i, cols)
+            gather_x(i, cols)
             for z_cols in gates_after.get(step, []):
                 gate_chunk(z_cols)
 
@@ -175,22 +214,16 @@ def tile_list_gate_none_kernel(
                 nc.vector.tensor_tensor(result[:, part, cols], sums, gate[:, part, cols], MULT)
                 nc.sync.dma_start(out=out_v[:, part, cols], in_=result[:, part, cols])
 
-        last = spans(X_LAST_GATHERS)
-        for cols in last[:-1]:
-            gather(x_picked, x_planes, x_list, x_wgt, PACK - 1, cols)
-        for cols in x_spans[:-1]:
-            interleave(x_grouped, x_picked, cols)
-        multiply_chunk(x_spans[0])
-        gather(x_picked, x_planes, x_list, x_wgt, PACK - 1, last[-1])
-        interleave(x_grouped, x_picked, x_spans[-1])
-        multiply_chunk(x_spans[1])
-        finish(*x_banks[0])
-        multiply_chunk(x_spans[2])
-        finish(*x_banks[1])
-        multiply_chunk(x_spans[3])
-        finish(*x_banks[2])
-        finish(*x_banks[3])
-        multiply_chunk(x_spans[4])
-        for item in x_banks[4:-1]:
-            finish(*item)
+        for h in range(2):
+            gather_x(PACK - 2, halves[h])
+            for cols in x_spans[2 * h : 2 * h + 2]:
+                gather_x(PACK - 1, cols)
+                interleave_x(cols)
+                if cols == x_spans[2]:
+                    multiply_chunk(x_spans[0])
+        for c in range(1, len(x_spans)):
+            finish(*x_banks[2 * c - 2])
+            multiply_chunk(x_spans[c])
+            finish(*x_banks[2 * c - 1])
+        finish(*x_banks[-2])
         finish(*x_banks[-1], pieces=2)

@@ -112,7 +112,9 @@ def tile_list_gate_none_kernel(
         turned = psum.tile([P, P], F32, name="bank")
         nc.tensor.transpose(turned[:], seed[:], ident[:])
         by_block = turned[:].rearrange("c (s g b) -> c s b g", s=2, g=HEADS)
-        x_wgt = [x_picked[1][:, PACK - 2, :], x_wgt_late[:]]
+        early_at = (PACK - 2) * HALF - X_CHUNKS[0]
+        late_flat = x_picked[1][:].rearrange("p i c -> p (i c)")
+        x_wgt = [late_flat[:, early_at : early_at + HALF], x_wgt_late[:]]
         for s, weights in enumerate(([z_wgt[:, cols] for cols in halves], x_wgt)):
             for blocks in spans([BLOCKS // 2] * 2):
                 nc.scalar.copy(
@@ -191,7 +193,7 @@ def tile_list_gate_none_kernel(
             interleave(z_grouped, z_picked, cols)
         gate_chunk(z_spans[0])
 
-        x_early = [(i, cols) for i in range(PACK - 2) for cols in halves]
+        x_early = [(0, halves[0]), (0, halves[1]), (1, halves[0])]
         gates_after = {0: z_spans[1:2], 1: z_spans[2:4]}
         for step, (i, cols) in enumerate(x_early):
             gather_x(i, cols)
@@ -214,16 +216,23 @@ def tile_list_gate_none_kernel(
                 nc.vector.tensor_tensor(result[:, part, cols], sums, gate[:, part, cols], MULT)
                 nc.sync.dma_start(out=out_v[:, part, cols], in_=result[:, part, cols])
 
-        for h in range(2):
-            gather_x(PACK - 2, halves[h])
-            for cols in x_spans[2 * h : 2 * h + 2]:
-                gather_x(PACK - 1, cols)
-                interleave_x(cols)
-                if cols == x_spans[2]:
-                    multiply_chunk(x_spans[0])
-        for c in range(1, len(x_spans)):
-            finish(*x_banks[2 * c - 2])
-            multiply_chunk(x_spans[c])
-            finish(*x_banks[2 * c - 1])
-        finish(*x_banks[-2])
+        gather_x(2, halves[0])
+        for cols in x_spans[:2]:
+            gather_x(3, cols)
+            interleave_x(cols)
+        gather_x(1, halves[1])
+        multiply_chunk(x_spans[0])
+        gather_x(2, halves[1])
+        multiply_chunk(x_spans[1])
+        for cols in x_spans[2:]:
+            gather_x(3, cols)
+            interleave_x(cols)
+        finish(*x_banks[0])
+        finish(*x_banks[1])
+        multiply_chunk(x_spans[2])
+        finish(*x_banks[2])
+        finish(*x_banks[3])
+        multiply_chunk(x_spans[3])
+        for item in x_banks[4:-1]:
+            finish(*item)
         finish(*x_banks[-1], pieces=2)

@@ -23,8 +23,9 @@ N_TILES = N // P
 BANK = 512
 HALF = J // 2
 Z_CHUNKS = [256, 256, 256, 256]
-X_CHUNKS = [256, 256, 256, 256]
-Z_FIRST_GATHERS = [256, 256, 512]
+X_CHUNKS = [128, 128, 256, 256, 256]
+X_LAST_GATHERS = [128, 384, 256, 256]
+Z_FIRST_GATHERS = [128, 128, 256, 512]
 HEADS = 8
 GROUP = P // HEADS
 BLOCKS = J // P
@@ -40,6 +41,7 @@ def tile_list_gate_none_kernel(
 ):
     nc = tc.nc
     halves = spans([HALF, HALF])
+    x_spans = spans(X_CHUNKS)
     out_v = out.rearrange("(t p) j -> p t j", p=P)
 
     with ExitStack() as ctx:
@@ -64,7 +66,6 @@ def tile_list_gate_none_kernel(
         wb_codes = keep.tile([P, 4 * N], U8, name="wb_codes", align_bytes=64)
         wa_scale = keep.tile([P, N], U8, name="wa_scale", align_bytes=64)
         wb_scale = keep.tile([P, N], U8, name="wb_scale", align_bytes=64)
-        z_head = keep.tile([P, Z_FIRST_GATHERS[0]], F32, name="z_head")
         seed = keep.tile([P, P], F32, name="seed")
         ident = keep.tile([P, P], F32, name="ident")
         spread = keep.tile([P, BLOCKS, HEADS, GROUP], F32, name="spread")
@@ -92,10 +93,8 @@ def tile_list_gate_none_kernel(
             rows = source.rearrange("(g r) (b c) -> r g b c", r=GROUP, c=P)[0]
             nc.sync.dma_start(out=seed[64 * s : 64 * (s + 1), :], in_=rows)
         nc.scalar.activation(warm[:, 8:9], warm[:, 0:1], SIGMOID)
-        nc.sync.dma_start(out=z_planes[0][:], in_=z_rows[:, 0, :])
         nc.sync.dma_start(z_list[:], offs2)
-        nc.sync.dma_start(out=z_head[:], in_=wgt2[:, first[0]])
-        for i in range(1, PACK):
+        for i in range(PACK):
             nc.sync.dma_start(out=z_planes[i][:], in_=z_rows[:, i, :])
         nc.sync.dma_start(x_list[:], offs)
         nc.sync.dma_start(out=x_planes[0][:], in_=x_rows[:, 0, :])
@@ -112,24 +111,31 @@ def tile_list_gate_none_kernel(
         turned = psum.tile([P, P], F32, name="bank")
         nc.tensor.transpose(turned[:], seed[:], ident[:])
         by_block = turned[:].rearrange("c (s g b) -> c s b g", s=2, g=HEADS)
-        early_at = (PACK - 2) * HALF - X_CHUNKS[0]
+        early_at = (PACK - 2) * HALF - X_LAST_GATHERS[0]
         late_flat = x_picked[1][:].rearrange("p i c -> p (i c)")
         x_wgt = [late_flat[:, early_at : early_at + HALF], x_wgt_late[:]]
-        for s, weights in enumerate(([z_wgt[:, cols] for cols in halves], x_wgt)):
-            for blocks in spans([BLOCKS // 2] * 2):
-                nc.scalar.copy(
+        streams = (
+            (first, [z_wgt[:, cols] for cols in first], nc.vector.tensor_copy),
+            (halves, x_wgt, nc.scalar.copy),
+        )
+        for s, (pieces, targets, expand) in enumerate(streams):
+            for cols in pieces:
+                blocks = slice(cols.start // P, cols.stop // P)
+                count = blocks.stop - blocks.start
+                expand(
                     spread[:, blocks],
-                    by_block[:, s, blocks].unsqueeze(3).to_broadcast([P, BLOCKS // 2, HEADS, GROUP]),
+                    by_block[:, s, blocks].unsqueeze(3).to_broadcast([P, count, HEADS, GROUP]),
                 )
-            for h, blocks in enumerate(spans([BLOCKS // 2] * 2)):
-                bank = psum.tile([P, BLOCKS // 2, P], F32, name="bank")
-                for b in range(blocks.start, blocks.stop):
+            for cols, target in zip(pieces, targets):
+                count = (cols.stop - cols.start) // P
+                bank = psum.tile([P, count, P], F32, name="bank")
+                for b in range(count):
                     nc.tensor.transpose(
-                        bank[:, b - blocks.start, :],
-                        spread[:, b].rearrange("c g r -> c (g r)"),
+                        bank[:, b, :],
+                        spread[:, cols.start // P + b].rearrange("c g r -> c (g r)"),
                         ident[:],
                     )
-                nc.scalar.copy(weights[h], bank[:].rearrange("p b c -> p (b c)"))
+                nc.scalar.copy(target, bank[:].rearrange("p b c -> p (b c)"))
 
         def gather(picked, planes, lists, weights, i, cols, base=0):
             window = planes[i][:].indirect(lists[:, cols.start // 16 : cols.stop // 16])
@@ -183,9 +189,8 @@ def tile_list_gate_none_kernel(
             for bank, tiles in project(wb_codes, FP8X4, wb_scale, z_codes, z_scale, cols):
                 nc.scalar.activation(gate[:, tiles, cols], bank[:], SIGMOID)
 
-        gather(z_picked, z_planes, z_list, z_head, 0, first[0])
         for i in range(PACK - 1):
-            for cols in first[1:] if i == 0 else [slice(0, J)]:
+            for cols in first if i == 0 else [slice(0, J)]:
                 gather(z_picked, z_planes, z_list, z_wgt, i, cols)
         z_spans = spans(Z_CHUNKS)
         for cols in z_spans:
@@ -193,14 +198,13 @@ def tile_list_gate_none_kernel(
             interleave(z_grouped, z_picked, cols)
         gate_chunk(z_spans[0])
 
-        x_early = [(0, halves[0]), (0, halves[1]), (1, halves[0])]
+        x_early = [(0, halves[0]), (0, halves[1]), (1, halves[0]), (1, x_spans[3])]
         gates_after = {0: z_spans[1:2], 1: z_spans[2:4]}
         for step, (i, cols) in enumerate(x_early):
             gather_x(i, cols)
             for z_cols in gates_after.get(step, []):
                 gate_chunk(z_cols)
 
-        x_spans = spans(X_CHUNKS)
         x_banks = []
 
         def multiply_chunk(cols):
@@ -216,23 +220,26 @@ def tile_list_gate_none_kernel(
                 nc.vector.tensor_tensor(result[:, part, cols], sums, gate[:, part, cols], MULT)
                 nc.sync.dma_start(out=out_v[:, part, cols], in_=result[:, part, cols])
 
-        gather_x(2, halves[0])
-        for cols in x_spans[:2]:
-            gather_x(3, cols)
-            interleave_x(cols)
-        gather_x(1, halves[1])
-        multiply_chunk(x_spans[0])
-        gather_x(2, halves[1])
-        multiply_chunk(x_spans[1])
-        for cols in x_spans[2:]:
-            gather_x(3, cols)
-            interleave_x(cols)
+        last = spans(X_LAST_GATHERS)
+        gather_x(PACK - 2, halves[0])
+        gather_x(PACK - 1, last[0])
+        interleave_x(x_spans[0])
+        gather_x(PACK - 1, last[1])
+        interleave_x(x_spans[1])
+        interleave_x(x_spans[2])
+        gather_x(1, x_spans[4])
+        gather_x(PACK - 2, halves[1])
+        for c in range(2):
+            multiply_chunk(x_spans[c])
+            gather_x(PACK - 1, last[2 + c])
+            interleave_x(x_spans[3 + c])
+        multiply_chunk(x_spans[2])
         finish(*x_banks[0])
         finish(*x_banks[1])
-        multiply_chunk(x_spans[2])
+        multiply_chunk(x_spans[3])
         finish(*x_banks[2])
         finish(*x_banks[3])
-        multiply_chunk(x_spans[3])
+        multiply_chunk(x_spans[4])
         for item in x_banks[4:-1]:
             finish(*item)
         finish(*x_banks[-1], pieces=2)

@@ -66,7 +66,7 @@ def tile_list_gate_none_kernel(
         wb_codes = keep.tile([P, 4 * N], U8, name="wb_codes", align_bytes=64)
         wa_scale = keep.tile([P, N], U8, name="wa_scale", align_bytes=64)
         wb_scale = keep.tile([P, N], U8, name="wb_scale", align_bytes=64)
-        seed = keep.tile([P, P], F32, name="seed")
+        seeds = [keep.tile([P, P], F32, name="seed%d" % s) for s in range(2)]
         ident = keep.tile([P, P], F32, name="ident")
         spread = keep.tile([P, BLOCKS, HEADS, GROUP], F32, name="spread")
         warm = keep.tile([P, 16], F32, name="warm")
@@ -89,12 +89,18 @@ def tile_list_gate_none_kernel(
         make_identity(nc, ident[:])
 
         first = spans(Z_FIRST_GATHERS)
-        for s, source in enumerate((wgt2, wgt)):
+
+        def load_seed(seed, source):
+            nc.vector.memset(seed[HEADS * BLOCKS :, :], 0.0)
             rows = source.rearrange("(g r) (b c) -> r g b c", r=GROUP, c=P)[0]
-            nc.sync.dma_start(out=seed[64 * s : 64 * (s + 1), :], in_=rows)
+            nc.sync.dma_start(out=seed[: HEADS * BLOCKS, :], in_=rows)
+
+        load_seed(seeds[0], wgt2)
         nc.scalar.activation(warm[:, 8:9], warm[:, 0:1], SIGMOID)
+        nc.sync.dma_start(out=z_planes[0][:], in_=z_rows[:, 0, :])
         nc.sync.dma_start(z_list[:], offs2)
-        for i in range(PACK):
+        load_seed(seeds[1], wgt)
+        for i in range(1, PACK):
             nc.sync.dma_start(out=z_planes[i][:], in_=z_rows[:, i, :])
         nc.sync.dma_start(x_list[:], offs)
         nc.sync.dma_start(out=x_planes[0][:], in_=x_rows[:, 0, :])
@@ -108,9 +114,6 @@ def tile_list_gate_none_kernel(
         nc.sync.dma_start(out=wa_codes[:].bitcast(I32), in_=wa_words[0].bitcast(I32))
         load_scales(nc.sync, wa_scale, wa_scales)
 
-        turned = psum.tile([P, P], F32, name="bank")
-        nc.tensor.transpose(turned[:], seed[:], ident[:])
-        by_block = turned[:].rearrange("c (s g b) -> c s b g", s=2, g=HEADS)
         early_at = (PACK - 2) * HALF - X_LAST_GATHERS[0]
         late_flat = x_picked[1][:].rearrange("p i c -> p (i c)")
         x_wgt = [late_flat[:, early_at : early_at + HALF], x_wgt_late[:]]
@@ -118,13 +121,16 @@ def tile_list_gate_none_kernel(
             (first, [z_wgt[:, cols] for cols in first], nc.vector.tensor_copy),
             (halves, x_wgt, nc.scalar.copy),
         )
-        for s, (pieces, targets, expand) in enumerate(streams):
+        for seed, (pieces, targets, expand) in zip(seeds, streams):
+            turned = psum.tile([P, P], F32, name="bank")
+            nc.tensor.transpose(turned[:], seed[:], ident[:])
+            by_block = turned[:, : HEADS * BLOCKS].rearrange("c (g b) -> c b g", g=HEADS)
             for cols in pieces:
                 blocks = slice(cols.start // P, cols.stop // P)
                 count = blocks.stop - blocks.start
                 expand(
                     spread[:, blocks],
-                    by_block[:, s, blocks].unsqueeze(3).to_broadcast([P, count, HEADS, GROUP]),
+                    by_block[:, blocks].unsqueeze(3).to_broadcast([P, count, HEADS, GROUP]),
                 )
             for cols, target in zip(pieces, targets):
                 count = (cols.stop - cols.start) // P
@@ -238,8 +244,7 @@ def tile_list_gate_none_kernel(
         finish(*x_banks[1])
         multiply_chunk(x_spans[3])
         finish(*x_banks[2])
-        finish(*x_banks[3])
         multiply_chunk(x_spans[4])
-        for item in x_banks[4:-1]:
+        for item in x_banks[3:-1]:
             finish(*item)
         finish(*x_banks[-1], pieces=2)

@@ -190,15 +190,24 @@ def tile_list_gate_none_kernel(
                 banks.append((bank, slice(t0, t0 + per_bank)))
             return banks
 
+        z_spans = spans(Z_CHUNKS)
+        late_gate = late_flat[:, :J].rearrange("p (t c) -> p t c", t=N_TILES)
+        late_banks = []
+
+        def gate_of(tiles, cols):
+            return late_gate[:, tiles, :] if cols == z_spans[-1] else gate[:, tiles, cols]
+
         def gate_chunk(cols):
             quantize(z_codes, z_scale, z_grouped, cols)
             for bank, tiles in project(wb_codes, FP8X4, wb_scale, z_codes, z_scale, cols):
-                nc.scalar.activation(gate[:, tiles, cols], bank[:], SIGMOID)
+                if cols == z_spans[-1]:
+                    late_banks.append((bank, tiles))
+                else:
+                    nc.scalar.activation(gate[:, tiles, cols], bank[:], SIGMOID)
 
         for i in range(PACK - 1):
             for cols in first if i == 0 else [slice(0, J)]:
                 gather(z_picked, z_planes, z_list, z_wgt, i, cols)
-        z_spans = spans(Z_CHUNKS)
         for cols in z_spans:
             gather(z_picked, z_planes, z_list, z_wgt, PACK - 1, cols)
             interleave(z_grouped, z_picked, cols)
@@ -223,7 +232,7 @@ def tile_list_gate_none_kernel(
             for t0 in range(tiles.start, tiles.stop, step):
                 part = slice(t0, t0 + step)
                 sums = bank[:, t0 - tiles.start : t0 - tiles.start + step, :]
-                nc.vector.tensor_tensor(result[:, part, cols], sums, gate[:, part, cols], MULT)
+                nc.vector.tensor_tensor(result[:, part, cols], sums, gate_of(part, cols), MULT)
                 nc.sync.dma_start(out=out_v[:, part, cols], in_=result[:, part, cols])
 
         last = spans(X_LAST_GATHERS)
@@ -239,6 +248,8 @@ def tile_list_gate_none_kernel(
             multiply_chunk(x_spans[c])
             gather_x(PACK - 1, last[2 + c])
             interleave_x(x_spans[3 + c])
+        for bank, tiles in late_banks:
+            nc.scalar.activation(gate_of(tiles, z_spans[-1]), bank[:], SIGMOID)
         multiply_chunk(x_spans[2])
         finish(*x_banks[0])
         finish(*x_banks[1])

@@ -151,8 +151,8 @@ def tile_list_gate_none_kernel(
         def interleave(grouped, picked, cols, base=0):
             local = slice(cols.start - base, cols.stop - base)
             nc.scalar.copy(
-                grouped[:, cols, :].rearrange("p (c e) i -> p c i e", e=4),
-                picked[:, :, local].rearrange("p i (c e) -> p c i e", e=4),
+                grouped[:, cols, :].rearrange("p (c e) i -> p c i e", e=2),
+                picked[:, :, local].rearrange("p i (c e) -> p c i e", e=2),
             )
 
         def gather_x(i, cols):

@@ -52,8 +52,8 @@ def tile_list_gate_none_kernel(
         z_list = keep.tile([P, J // 16], U16, name="z_list")
         x_wgt_late = keep.tile([P, HALF], F32, name="x_wgt_late")
         z_wgt = keep.tile([P, J], F32, name="z_wgt")
-        x_planes = [keep.tile([P, T], F32, name="x_plane%d" % i) for i in range(PACK)]
-        z_planes = [keep.tile([P, T], F32, name="z_plane%d" % i) for i in range(PACK)]
+        x_planes = [keep.tile([P, T], F32, name="x_plane%d" % i, align_bytes=256) for i in range(PACK)]
+        z_planes = [keep.tile([P, T], F32, name="z_plane%d" % i, align_bytes=256) for i in range(PACK)]
         x_picked = [keep.tile([P, PACK, HALF], F32, name="x_picked%d" % h) for h in range(2)]
         z_picked = keep.tile([P, PACK, J], F32, name="z_picked")
         x_grouped = keep.tile([P, J, PACK], BF16, name="x_grouped", align_bytes=64)
@@ -62,16 +62,16 @@ def tile_list_gate_none_kernel(
         z_codes = keep.tile([P, J], U32, name="z_codes", align_bytes=64)
         x_scale = keep.tile([P, J], U8, name="x_scale", align_bytes=64)
         z_scale = keep.tile([P, J], U8, name="z_scale", align_bytes=64)
-        wa_codes = keep.tile([P, 2 * N], U8, name="wa_codes", align_bytes=64)
-        wb_codes = keep.tile([P, 4 * N], U8, name="wb_codes", align_bytes=64)
-        wa_scale = keep.tile([P, N], U8, name="wa_scale", align_bytes=64)
-        wb_scale = keep.tile([P, N], U8, name="wb_scale", align_bytes=64)
-        seeds = [keep.tile([P, P], F32, name="seed%d" % s) for s in range(2)]
+        wa_codes = keep.tile([P, 2 * N], U8, name="wa_codes", align_bytes=256)
+        wb_codes = keep.tile([P, 4 * N], U8, name="wb_codes", align_bytes=256)
+        wa_scale = keep.tile([P, N], U8, name="wa_scale", align_bytes=256)
+        wb_scale = keep.tile([P, N], U8, name="wb_scale", align_bytes=256)
+        seeds = [keep.tile([P, P], F32, name="seed%d" % s, align_bytes=256) for s in range(2)]
         ident = keep.tile([P, P], F32, name="ident")
         spread = keep.tile([P, BLOCKS, HEADS, GROUP], F32, name="spread")
         warm = keep.tile([P, 16], F32, name="warm")
         gate = keep.tile([P, N_TILES, J], F32, name="gate")
-        result = keep.tile([P, N_TILES, J], F32, name="result")
+        result = keep.tile([P, N_TILES, J], F32, name="result", align_bytes=256)
 
         x_rows = xT.rearrange("(p i) t -> p i t", i=PACK)
         z_rows = zT.rearrange("(p i) t -> p i t", i=PACK)

@@ -23,7 +23,7 @@ N_TILES = N // P
 BANK = 512
 HALF = J // 2
 Z_CHUNKS = [256, 256, 256, 256]
-X_CHUNKS = [128, 128, 256, 256, 256]
+X_CHUNKS = [128, 256, 128, 256, 256]
 X_LAST_GATHERS = [128, 384, 256, 256]
 Z_FIRST_GATHERS = [128, 128, 256, 512]
 HEADS = 8
@@ -54,7 +54,13 @@ def tile_list_gate_none_kernel(
         z_wgt = keep.tile([P, J], F32, name="z_wgt")
         x_planes = [keep.tile([P, T], F32, name="x_plane%d" % i, align_bytes=256) for i in range(PACK)]
         z_planes = [keep.tile([P, T], F32, name="z_plane%d" % i, align_bytes=256) for i in range(PACK)]
-        x_picked = [keep.tile([P, PACK, HALF], F32, name="x_picked%d" % h) for h in range(2)]
+        early_picks_at = (PACK - 1) * HALF - X_CHUNKS[0]
+        x_picks = keep.tile([P, early_picks_at + PACK * HALF], F32, name="x_picks")
+        late_flat = x_picks[:, : PACK * HALF]
+        x_picked = [
+            flat.rearrange("p (i c) -> p i c", i=PACK)
+            for flat in (x_picks[:, early_picks_at:], late_flat)
+        ]
         z_picked = keep.tile([P, PACK, J], F32, name="z_picked")
         x_grouped = keep.tile([P, J, PACK], BF16, name="x_grouped", align_bytes=64)
         z_grouped = keep.tile([P, J, PACK], BF16, name="z_grouped", align_bytes=64)
@@ -115,7 +121,6 @@ def tile_list_gate_none_kernel(
         load_scales(nc.sync, wa_scale, wa_scales)
 
         early_at = (PACK - 2) * HALF - X_LAST_GATHERS[0]
-        late_flat = x_picked[1][:].rearrange("p i c -> p (i c)")
         x_wgt = [late_flat[:, early_at : early_at + HALF], x_wgt_late[:]]
         streams = (
             (first, [z_wgt[:, cols] for cols in first], nc.vector.tensor_copy),
@@ -243,17 +248,17 @@ def tile_list_gate_none_kernel(
         interleave_x(x_spans[1])
         interleave_x(x_spans[2])
         gather_x(1, x_spans[4])
+        multiply_chunk(x_spans[0])
         gather_x(PACK - 2, halves[1])
         for c in range(2):
-            multiply_chunk(x_spans[c])
+            multiply_chunk(x_spans[1 + c])
             gather_x(PACK - 1, last[2 + c])
             interleave_x(x_spans[3 + c])
         for bank, tiles in late_banks:
             nc.scalar.activation(gate_of(tiles, z_spans[-1]), bank[:], SIGMOID)
-        multiply_chunk(x_spans[2])
         finish(*x_banks[0])
-        finish(*x_banks[1])
         multiply_chunk(x_spans[3])
+        finish(*x_banks[1])
         finish(*x_banks[2])
         multiply_chunk(x_spans[4])
         for item in x_banks[3:-1]:

@@ -260,7 +260,7 @@ def tile_list_gate_none_kernel(
         multiply_chunk(x_spans[3])
         finish(*x_banks[1])
         finish(*x_banks[2])
+        finish(*x_banks[3])
         multiply_chunk(x_spans[4])
-        for item in x_banks[3:-1]:
-            finish(*item)
-        finish(*x_banks[-1], pieces=2)
+        for item in x_banks[4:]:
+            finish(*item, pieces=2)

@@ -262,5 +262,6 @@ def tile_list_gate_none_kernel(
         finish(*x_banks[2])
         finish(*x_banks[3])
         multiply_chunk(x_spans[4])
-        for item in x_banks[4:]:
-            finish(*item, pieces=2)
+        for item in x_banks[4:-1]:
+            finish(*item)
+        finish(*x_banks[-1], pieces=2)

from contextlib import ExitStack

import concourse.mybir as mybir
from concourse.masks import make_identity

K, N, T, J = 512, 512, 2048, 1024
FLOPS = 2 * 2 * K * N * J

F32 = mybir.dt.float32
BF16 = mybir.dt.bfloat16
I32 = mybir.dt.int32
U32 = mybir.dt.uint32
U16 = mybir.dt.uint16
U8 = mybir.dt.uint8
FP8X4 = mybir.dt.float8_e4m3fn_x4
FP4X4 = mybir.dt.float4_e2m1fn_x4
MULT = mybir.AluOpType.mult
SIGMOID = mybir.ActivationFunctionType.Sigmoid

P = 128
PACK = 4
N_TILES = N // P
BANK = 512
HALF = J // 2
Z_CHUNKS = [256, 256, 256, 256]
X_CHUNKS = [128, 256, 128, 256, 256]
X_LAST_GATHERS = [128, 384, 256, 256]
Z_FIRST_GATHERS = [128, 128, 256, 512]
HEADS = 8
GROUP = P // HEADS
BLOCKS = J // P


def spans(widths):
    starts = [sum(widths[:i]) for i in range(len(widths))]
    return [slice(s, s + w) for s, w in zip(starts, widths)]


def tile_list_gate_none_kernel(
    tc, xT, wgt, zT, wgt2, wa_words, wa_scales, wb_words, wb_scales, offs, offs2, out
):
    nc = tc.nc
    halves = spans([HALF, HALF])
    x_spans = spans(X_CHUNKS)
    out_v = out.rearrange("(t p) j -> p t j", p=P)

    with ExitStack() as ctx:
        keep = ctx.enter_context(tc.tile_pool(name="keep", bufs=1))
        psum = ctx.enter_context(tc.psum_pool(name="psum", bufs=8))

        x_list = keep.tile([P, J // 16], U16, name="x_list")
        z_list = keep.tile([P, J // 16], U16, name="z_list")
        x_wgt_late = keep.tile([P, HALF], F32, name="x_wgt_late")
        z_wgt = keep.tile([P, J], F32, name="z_wgt")
        x_planes = [keep.tile([P, T], F32, name="x_plane%d" % i, align_bytes=256) for i in range(PACK)]
        z_planes = [keep.tile([P, T], F32, name="z_plane%d" % i, align_bytes=256) for i in range(PACK)]
        early_picks_at = (PACK - 1) * HALF - X_CHUNKS[0]
        x_picks = keep.tile([P, early_picks_at + PACK * HALF], F32, name="x_picks")
        late_flat = x_picks[:, : PACK * HALF]
        x_picked = [
            flat.rearrange("p (i c) -> p i c", i=PACK)
            for flat in (x_picks[:, early_picks_at:], late_flat)
        ]
        z_picked = keep.tile([P, PACK, J], F32, name="z_picked")
        x_grouped = keep.tile([P, J, PACK], BF16, name="x_grouped", align_bytes=64)
        z_grouped = keep.tile([P, J, PACK], BF16, name="z_grouped", align_bytes=64)
        x_codes = keep.tile([P, J], U32, name="x_codes", align_bytes=64)
        z_codes = keep.tile([P, J], U32, name="z_codes", align_bytes=64)
        x_scale = keep.tile([P, J], U8, name="x_scale", align_bytes=64)
        z_scale = keep.tile([P, J], U8, name="z_scale", align_bytes=64)
        wa_codes = keep.tile([P, 2 * N], U8, name="wa_codes", align_bytes=256)
        wb_codes = keep.tile([P, 4 * N], U8, name="wb_codes", align_bytes=256)
        wa_scale = keep.tile([P, N], U8, name="wa_scale", align_bytes=256)
        wb_scale = keep.tile([P, N], U8, name="wb_scale", align_bytes=256)
        seeds = [keep.tile([P, P], F32, name="seed%d" % s, align_bytes=256) for s in range(2)]
        ident = keep.tile([P, P], F32, name="ident")
        spread = keep.tile([P, BLOCKS, HEADS, GROUP], F32, name="spread")
        warm = keep.tile([P, 16], F32, name="warm")
        gate = keep.tile([P, N_TILES, J], F32, name="gate")
        result = keep.tile([P, N_TILES, J], F32, name="result", align_bytes=256)

        x_rows = xT.rearrange("(p i) t -> p i t", i=PACK)
        z_rows = zT.rearrange("(p i) t -> p i t", i=PACK)

        def load_scales(queue, plane, rows):
            for q in range(4):
                queue.dma_start(
                    out=plane[32 * q : 32 * q + 4, :].bitcast(I32),
                    in_=rows[0, 4 * q : 4 * q + 4, :].bitcast(I32),
                )

        nc.vector.memset(wb_scale[:].bitcast(I32), 0)
        nc.vector.memset(wa_scale[:].bitcast(I32), 0)
        nc.vector.memset(warm[:, 0:1], 0.0)
        make_identity(nc, ident[:])

        first = spans(Z_FIRST_GATHERS)

        def load_seed(seed, source):
            nc.vector.memset(seed[HEADS * BLOCKS :, :], 0.0)
            rows = source.rearrange("(g r) (b c) -> r g b c", r=GROUP, c=P)[0]
            nc.sync.dma_start(out=seed[: HEADS * BLOCKS, :], in_=rows)

        load_seed(seeds[0], wgt2)
        nc.scalar.activation(warm[:, 8:9], warm[:, 0:1], SIGMOID)
        nc.sync.dma_start(out=z_planes[0][:], in_=z_rows[:, 0, :])
        nc.sync.dma_start(z_list[:], offs2)
        load_seed(seeds[1], wgt)
        for i in range(1, PACK):
            nc.sync.dma_start(out=z_planes[i][:], in_=z_rows[:, i, :])
        nc.sync.dma_start(x_list[:], offs)
        nc.sync.dma_start(out=x_planes[0][:], in_=x_rows[:, 0, :])
        nc.sync.dma_start(
            out=wb_codes[:].bitcast(I32),
            in_=wb_words[0].rearrange("p n t -> p (n t)").bitcast(I32),
        )
        load_scales(nc.sync, wb_scale, wb_scales)
        for i in range(1, PACK):
            nc.sync.dma_start(out=x_planes[i][:], in_=x_rows[:, i, :])
        nc.sync.dma_start(out=wa_codes[:].bitcast(I32), in_=wa_words[0].bitcast(I32))
        load_scales(nc.sync, wa_scale, wa_scales)

        early_at = (PACK - 2) * HALF - X_LAST_GATHERS[0]
        x_wgt = [late_flat[:, early_at : early_at + HALF], x_wgt_late[:]]
        streams = (
            (first, [z_wgt[:, cols] for cols in first], nc.vector.tensor_copy),
            (halves, x_wgt, nc.scalar.copy),
        )
        for seed, (pieces, targets, expand) in zip(seeds, streams):
            turned = psum.tile([P, P], F32, name="bank")
            nc.tensor.transpose(turned[:], seed[:], ident[:])
            by_block = turned[:, : HEADS * BLOCKS].rearrange("c (g b) -> c b g", g=HEADS)
            for cols in pieces:
                blocks = slice(cols.start // P, cols.stop // P)
                count = blocks.stop - blocks.start
                expand(
                    spread[:, blocks],
                    by_block[:, blocks].unsqueeze(3).to_broadcast([P, count, HEADS, GROUP]),
                )
            for cols, target in zip(pieces, targets):
                count = (cols.stop - cols.start) // P
                bank = psum.tile([P, count, P], F32, name="bank")
                for b in range(count):
                    nc.tensor.transpose(
                        bank[:, b, :],
                        spread[:, cols.start // P + b].rearrange("c g r -> c (g r)"),
                        ident[:],
                    )
                nc.scalar.copy(target, bank[:].rearrange("p b c -> p (b c)"))

        def gather(picked, planes, lists, weights, i, cols, base=0):
            window = planes[i][:].indirect(lists[:, cols.start // 16 : cols.stop // 16])
            local = slice(cols.start - base, cols.stop - base)
            nc.vector.tensor_tensor(picked[:, i, local], window, weights[:, local], MULT)

        def interleave(grouped, picked, cols, base=0):
            local = slice(cols.start - base, cols.stop - base)
            nc.scalar.copy(
                grouped[:, cols, :].rearrange("p (c e) i -> p c i e", e=2),
                picked[:, :, local].rearrange("p i (c e) -> p c i e", e=2),
            )

        def gather_x(i, cols):
            h = cols.start // HALF
            gather(x_picked[h], x_planes, x_list, x_wgt[h], i, cols, h * HALF)

        def interleave_x(cols):
            h = cols.start // HALF
            interleave(x_grouped, x_picked[h], cols, h * HALF)

        def quantize(codes, scale, grouped, cols):
            nc.vector.quantize_mx(
                out=codes[:, cols].bitcast(FP8X4),
                scales=scale[:, cols],
                in_=grouped[:, cols, :].rearrange("p c i -> p (c i)"),
            )

        def project(w_codes, w_dtype, w_scale, codes, scale, cols):
            width = cols.stop - cols.start
            per_bank = BANK // width
            w_bytes = w_codes.shape[1] // N_TILES
            banks = []
            for t0 in range(0, N_TILES, per_bank):
                bank = psum.tile([P, per_bank, width], F32, name="bank")
                for t in range(t0, t0 + per_bank):
                    nc.tensor.matmul_mx(
                        out=bank[:, t - t0, :],
                        lhsT=w_codes[:, t * w_bytes : (t + 1) * w_bytes].bitcast(w_dtype),
                        lhsT_scale=w_scale[:, t * P : (t + 1) * P],
                        rhs=codes[:, cols].bitcast(FP8X4),
                        rhs_scale=scale[:, cols],
                        start=True,
                        stop=True,
                    )
                banks.append((bank, slice(t0, t0 + per_bank)))
            return banks

        z_spans = spans(Z_CHUNKS)
        late_gate = late_flat[:, :J].rearrange("p (t c) -> p t c", t=N_TILES)
        late_banks = []

        def gate_of(tiles, cols):
            return late_gate[:, tiles, :] if cols == z_spans[-1] else gate[:, tiles, cols]

        def gate_chunk(cols):
            quantize(z_codes, z_scale, z_grouped, cols)
            for bank, tiles in project(wb_codes, FP8X4, wb_scale, z_codes, z_scale, cols):
                if cols == z_spans[-1]:
                    late_banks.append((bank, tiles))
                else:
                    nc.scalar.activation(gate[:, tiles, cols], bank[:], SIGMOID)

        for i in range(PACK - 1):
            for cols in first if i == 0 else [slice(0, J)]:
                gather(z_picked, z_planes, z_list, z_wgt, i, cols)
        for cols in z_spans:
            gather(z_picked, z_planes, z_list, z_wgt, PACK - 1, cols)
            interleave(z_grouped, z_picked, cols)
        gate_chunk(z_spans[0])

        x_early = [(0, halves[0]), (0, halves[1]), (1, halves[0]), (1, x_spans[3])]
        gates_after = {0: z_spans[1:2], 1: z_spans[2:4]}
        for step, (i, cols) in enumerate(x_early):
            gather_x(i, cols)
            for z_cols in gates_after.get(step, []):
                gate_chunk(z_cols)

        x_banks = []

        def multiply_chunk(cols):
            quantize(x_codes, x_scale, x_grouped, cols)
            for bank, tiles in project(wa_codes, FP4X4, wa_scale, x_codes, x_scale, cols):
                x_banks.append((bank, tiles, cols))

        def finish(bank, tiles, cols, pieces=1):
            step = (tiles.stop - tiles.start) // pieces
            for t0 in range(tiles.start, tiles.stop, step):
                part = slice(t0, t0 + step)
                sums = bank[:, t0 - tiles.start : t0 - tiles.start + step, :]
                nc.vector.tensor_tensor(result[:, part, cols], sums, gate_of(part, cols), MULT)
                nc.sync.dma_start(out=out_v[:, part, cols], in_=result[:, part, cols])

        last = spans(X_LAST_GATHERS)
        gather_x(PACK - 2, halves[0])
        gather_x(PACK - 1, last[0])
        interleave_x(x_spans[0])
        gather_x(PACK - 1, last[1])
        interleave_x(x_spans[1])
        interleave_x(x_spans[2])
        gather_x(1, x_spans[4])
        multiply_chunk(x_spans[0])
        gather_x(PACK - 2, halves[1])
        for c in range(2):
            multiply_chunk(x_spans[1 + c])
            gather_x(PACK - 1, last[2 + c])
            interleave_x(x_spans[3 + c])
        for bank, tiles in late_banks:
            nc.scalar.activation(gate_of(tiles, z_spans[-1]), bank[:], SIGMOID)
        finish(*x_banks[0])
        multiply_chunk(x_spans[3])
        finish(*x_banks[1])
        finish(*x_banks[2])
        finish(*x_banks[3])
        multiply_chunk(x_spans[4])
        for item in x_banks[4:-1]:
            finish(*item)
        finish(*x_banks[-1], pieces=2)
